import numpy as np, ml_dtypes
CORES = [35,38,43,46]
N = 4
import mx_ref
BF = ml_dtypes.bfloat16
def entries(a):
    return np.ascontiguousarray(a.T).reshape(-1)
def table(e):
    return np.ascontiguousarray(np.reshape(e, (-1, 16)).T).astype(np.int32)
def cols(t, e):
    v = np.concatenate([t.reshape(128, -1, 4), np.zeros((128, 1, 4), BF)], axis=1)
    return np.ascontiguousarray(v[:, e]).reshape(128, -1)
def tile(rs):
    return np.stack(rs, axis=2).reshape(128, -1).astype(BF)
def cut(t, i, w=512):
    return t[:, w * i:w * i + w]
def f(rng, *shape):
    return mx_ref.flush((rng.standard_normal(shape, dtype=np.float32) * np.exp2(rng.integers(-2, 3, shape[:-1] + (1,)))).astype(BF))
def wide(rng, *shape, cols=0):
    v = rng.standard_normal(shape, dtype=np.float32) * np.exp2(rng.integers(-12, 13, shape)).astype(np.float32)
    if cols: v *= np.repeat(np.exp2(rng.integers(-cols, cols + 1, shape[:-2] + (1, shape[-1] // 4))) * (rng.random(shape[:-2] + (1, shape[-1] // 4)) > 0.0625), 4, axis=-1).astype(np.float32)
    return mx_ref.flush(v.astype(BF))
T, CAPA, CAPB, TR = 512, 160, 136, 40
def mix(rng, n, la=0, lb=0):
    n = n.copy()
    for _ in range(4000):
        p, q = rng.integers(0, N, (2, 3)); k = rng.integers(0, 4)
        p2, q2 = p.copy(), q.copy(); m = n.copy()
        if k == 3: p2[1] = q[1]
        else: p2[k], q2[k] = q[k], p[k]
        m[tuple(p)] -= 1; m[tuple(p2)] += 1
        if k < 3: m[tuple(q)] -= 1; m[tuple(q2)] += 1
        sa, ab = m.sum(axis=2), m.sum(axis=0)
        if m.min() >= 0 and m.max() <= TR and (sa <= CAPA).all() and (sa >= la).all() and (ab <= CAPB).all() and (ab >= lb).all(): n = m
    return n
def even():
    return np.full((N, N, N), T // N ** 2)
def places(rng, k, cap, by=None):
    out = np.zeros(len(k), int)
    for g in np.unique(k):
        j = np.flatnonzero(k == g)
        if by is None: out[j] = g * cap + rng.permutation(cap)[:len(j)]
        else: out[j[np.argsort(by[j])]] = g * cap + cap - 1 - np.arange(len(j))
    return out
def lists(rng, n, back=False):
    s, a, b = np.repeat(np.argwhere(n >= 0), n.reshape(-1), axis=0).T
    col = np.concatenate([rng.permutation(T) for r in range(N)])
    snd, pas, tri = np.full(N * N * CAPA, -1), np.full(N * N * CAPB, -1), np.full(N * N * N * TR, -1)
    p1 = places(rng, s * N + a, CAPA, col if back else None); snd[p1] = col
    arr = s * CAPA + p1 % CAPA
    p2 = places(rng, a * N + b, CAPB, arr if back else None); pas[p2] = arr
    p3 = places(rng, (s * N + a) * N + b, TR, col if back else None); tri[p3] = col
    c, t = a * CAPB + p2 % CAPB, (s * N + a) * TR + p3 % TR
    plc, plt = [], []
    for r in range(N):
        j = rng.permutation(np.flatnonzero(b == r))
        if back: j = j[np.argsort(-c[j])]
        plc.append(table(c[j])); plt.append(table(t[j]))
    return {"snd": np.stack([table(v) for v in snd.reshape(N, -1)]), "pas": np.stack([table(v) for v in pas.reshape(N, -1)]), "tri": np.stack([table(v) for v in tri.reshape(N, -1)]), "plc": np.stack(plc), "plt": np.stack(plt)}
def values(rng):
    return {"x": f(rng, N, 128, 4 * T), "w": f(rng, N, 128, 2048), "vv": f(rng, N, 128, 512)}
def setup_inputs(rng):
    return {**values(rng), **lists(rng, mix(rng, even()))}
def heavy(rng, d):
    n = even()
    for k in range(CAPB // N - T // N ** 2):
        for s in range(N):
            for a in range(N):
                n[s, a, (a + d) % N] += 1; n[s, a, (a + d + 1 + (s + k) % (N - 1)) % N] -= 1
    return {**values(rng), **lists(rng, mix(rng, n, lb=CAPB * np.roll(np.eye(N, dtype=int), d, axis=1)))}
def setup_inputs_diag(rng):
    return heavy(rng, 0)
def setup_inputs_onward(rng):
    return heavy(rng, int(rng.integers(1, N)))
def setup_inputs_full(rng):
    k = T // CAPA
    g = np.zeros((N, N), int); g[:, :k] = CAPA; g[:, k] = T - k * CAPA
    g = np.stack([np.roll(g[s], s) for s in range(N)])[rng.permutation(N)][:, rng.permutation(N)]
    return {**values(rng), **lists(rng, mix(rng, np.repeat(g[:, :, None] // N, N, axis=2), la=np.where(g == CAPA, CAPA, 0)))}
def setup_inputs_reversed(rng):
    return {**values(rng), **lists(rng, mix(rng, even()), back=True)}
def setup_inputs_spread(rng):
    d = setup_inputs(rng); d["x"] = wide(rng, N, 128, 4 * T); return d
def check_inputs(d):
    b = []
    snd, pas, tri, plc, plt = [[entries(d[k][r]) for r in range(N)] for k in ("snd", "pas", "tri", "plc", "plt")]
    for r in range(N):
        if snd[r].min() < -1 or not np.array_equal(np.sort(snd[r][snd[r] >= 0]), np.arange(T)): b.append("snd")
        if tri[r].min() < -1 or not np.array_equal(np.sort(tri[r][tri[r] >= 0]), np.arange(T)): b.append("tri")
        for a in range(N):
            u, v = snd[r][a * CAPA:(a + 1) * CAPA], tri[r][a * N * TR:(a + 1) * N * TR]
            if not np.array_equal(np.sort(u[u >= 0]), np.sort(v[v >= 0])): b.append("tri")
    arrived = [np.concatenate([snd[s][a * CAPA:(a + 1) * CAPA] for s in range(N)]) for a in range(N)]
    for a in range(N):
        if pas[a].min() < -1 or not np.array_equal(np.sort(pas[a][pas[a] >= 0]), np.flatnonzero(arrived[a] >= 0)): b.append("pas")
    if b: return b
    for r in range(N):
        k = np.concatenate([pas[a][r * CAPB:(r + 1) * CAPB] for a in range(N)])
        t = np.concatenate([tri[s][(a * N + r) * TR:(a * N + r + 1) * TR] for s in range(N) for a in range(N)])
        if not np.array_equal(np.sort(plc[r]), np.flatnonzero(k >= 0)): b.append("plc"); continue
        if not np.array_equal(np.sort(plt[r]), np.flatnonzero(t >= 0)): b.append("plt"); continue
        a, m = plc[r] // CAPB, k[plc[r]]
        if (plt[r] // TR != m // CAPA * N + a).any() or (t[plt[r]] != np.stack(arrived)[a, m]).any(): b.append("plt")
    return b
def reference(x, w, vv, snd, pas, tri, plc, plt):
    h = []
    for a in range(N):
        q = mx_ref.quantize(np.concatenate([cols(x[s], entries(snd[s])[a * CAPA:(a + 1) * CAPA]) for s in range(N)], axis=1))
        h.append(tile([np.maximum(mx_ref.matmul(mx_ref.quantize(cut(w[a], i)), q), np.float32(0)) * np.float32(0.043) for i in range(4)]))
    y = np.zeros((N, 128, T), np.float32)
    for b in range(N):
        t = np.concatenate([cols(h[a], entries(pas[a])[b * CAPB:(b + 1) * CAPB]) for a in range(N)], axis=1)
        y[b] = mx_ref.matmul(mx_ref.quantize(vv[b]), mx_ref.quantize(cols(t, entries(plc[b]))))
    return {"y": y}

@@ -1,0 +1,278 @@
+from concourse.bass import DstId, RemoteDMATransfer
+from concourse.mybir import dt, AluOpType, ActivationFunctionType
+
+N, TR = 4, 40
+C = N * TR
+H = 2 * TR
+W = N * C
+L = C // 16
+F8 = "float8_e4m3fn_x4"
+SCRATCH = {
+    "xb": ("sbuf", [128, 2048], "bfloat16"),
+    "wb": ("sbuf", [128, 2048], "bfloat16"),
+    "vb": ("sbuf", [128, 512], "bfloat16"),
+    "trl": ("sbuf", [128, 40], "int32"),
+    "plr": ("sbuf", [128, 32], "int32"),
+    "toff": ("sbuf", [128, 40], "uint16"),
+    "poff": ("sbuf", [128, 32], "uint16"),
+    "kf": ("sbuf", [128, 32], "float32"),
+    "xg": ("sbuf", [128, 4 * W], "bfloat16"),
+    "qx": ("sbuf", [128, W], F8),
+    "sx": ("sbuf", [128, W], "uint8"),
+    "re0": ("sbuf", [128, C], F8),
+    "rse0": ("sbuf", [128, C], "uint8"),
+    "re1": ("sbuf", [128, 2 * C], F8),
+    "rse1": ("sbuf", [128, 2 * C], "uint8"),
+    "wq": ("sbuf", [128, 512], F8),
+    "ws": ("sbuf", [128, 512], "uint8"),
+    "vq": ("sbuf", [128, 128], F8),
+    "vs": ("sbuf", [128, 128], "uint8"),
+    "ps": ("psum", [128, 4096], "float32"),
+    "ysb": ("sbuf", [128, W], "float32"),
+    "yo": ("sbuf", [128, 512], "float32"),
+}
+for _h in range(2):
+    SCRATCH.update({
+        "h%d" % _h: ("sbuf", [128, N, 4 * H], "bfloat16"),
+        "qf%d" % _h: ("sbuf", [128, 2 * H], F8),
+        "sf%d" % _h: ("sbuf", [128, 2 * H], "uint8"),
+        "qo%d" % _h: ("sbuf", [128, 3 * H], F8),
+        "so%d" % _h: ("sbuf", [128, 3 * H], "uint8"),
+        "lf%d" % _h: ("sbuf", [128, 2 * H], F8),
+        "lsf%d" % _h: ("sbuf", [128, 2 * H], "uint8"),
+    })
+for _j in range(13):
+    SCRATCH["t%d" % _j] = ("sbuf", [128, 32], "int32")
+SEMAPHORES = (["tl", "xl", "wl", "vl", "pl", "tof", "qw", "qv", "rf", "rn", "ls", "yd0", "yd1", "st"]
+              + ["g%d" % j for j in range(N)] + ["qx%d" % j for j in range(N)]
+              + ["qhf%d" % j for j in range(2)] + ["qho%d" % j for j in range(2)]
+              + ["k%d" % j for j in range(15)]
+              + ["m%d_%d" % (k, i) for k in range(N) for i in range(4)]
+              + ["r%d_%d" % (k, i) for k in range(2) for i in range(4)]
+              + ["ax%d" % j for j in range(N)] + ["ah%d_%d" % (h, j) for h in range(2) for j in range(N)]
+              + ["y%d" % j for j in range(N)] + ["c%d" % j for j in range(N)])
+
+
+def roles(T, topo, r):
+    me = T.cores[r]
+    far = [q for q in range(N) if topo.chip(T.cores[q]) != topo.chip(me)]
+    far.sort(key=lambda q: (q % 2 != r % 2, q))
+    near = [q for q in range(N) if q != r and q not in far][0]
+    out = topo.engines(me, T.cores[far[0]])
+    half = len(out) // 2
+    inside = [e for e in topo.engines(me, T.cores[near]) if e not in out]
+    hop1 = {far[0]: out, far[1]: out, near: inside}
+    hop2 = {far[0]: out[:half], far[1]: out[half:], near: inside}
+    return far, near, hop1, hop2
+
+
+def rank_program(g, core, T, topo):
+    r = T.rank_of(core)
+    if r is None:
+        return
+    S = T.sem
+    V, A, P = g.vector, g.scalar, g.tensor
+    Copy, Relu, M = ActivationFunctionType.Copy, ActivationFunctionType.Relu, AluOpType
+    far, near, hop1, hop2 = roles(T, topo, r)
+    early, late = far
+    f0, o0 = 2 * (far[0] // 2), 2 * (r // 2)
+    assert sorted(far) == [f0, f0 + 1] and sorted([r, near]) == [o0, o0 + 1]
+    odd = r % 2
+
+    for k in range(8):
+        q = g.sync if k < 4 else A
+        q.dma_start(T.trl[16 * k:16 * k + 16, :], T.tri[:]).then_inc(S["tl"], 16)
+    g.sync.dma_start(T.xb[:], T.x[:]).then_inc(S["xl"], 16)
+    g.sync.dma_start(T.wb[:], T.w[:]).then_inc(S["wl"], 16)
+    g.sync.dma_start(T.vb[:], T.vv[:]).then_inc(S["vl"], 16)
+    for k in range(8):
+        g.sync.dma_start(T.plr[16 * k:16 * k + 16, :], T.plt[:]).then_inc(S["pl"], 16)
+
+    V.wait_ge(S["tl"], 128)
+    V.tensor_scalar(T.toff[:], T.trl[:], 0.0, 4.0, M.max, M.mult).then_inc(S["tof"], 1)
+    for e in (V, A):
+        e.wait_ge(S["tof"], 1)
+        e.wait_ge(S["xl"], 16)
+
+    def gather(a, nv):
+        for t in range(4):
+            src = T.xb[:, t:2048].indirect(T.toff[:, a * L:(a + 1) * L])
+            dst = T.xg[:, a * 4 * C + t:(a + 1) * 4 * C:4]
+            if t < nv:
+                V.tensor_copy(dst, src).then_inc(S["g%d" % a], 1)
+            else:
+                A.activation(dst, src, Copy).then_inc(S["g%d" % a], 1)
+
+    def pack(a):
+        V.wait_ge(S["g%d" % a], 4)
+        V.quantize_mx(T.qx[:, a * C:(a + 1) * C], T.sx[:, a * C:(a + 1) * C],
+                      T.xg[:, a * 4 * C:(a + 1) * 4 * C]).then_inc(S["qx%d" % a], 1)
+
+    for a, nv in ((early, 2), (near, 2), (late, 1)):
+        gather(a, nv)
+        pack(a)
+    gather(r, 1)
+    V.wait_ge(S["wl"], 16)
+    V.quantize_mx(T.wq[:], T.ws[:], T.wb[:]).then_inc(S["qw"], 1)
+    pack(r)
+    V.wait_ge(S["vl"], 16)
+    V.quantize_mx(T.vq[:], T.vs[:], T.vb[:]).then_inc(S["qv"], 1)
+
+    def fire(qs, eng, sem, src, dst):
+        trs = []
+        for q in qs:
+            rid, pid = topo.addr(T.cores[q])[:2]
+            trs.append(RemoteDMATransfer(dst_ids=[DstId(rid=rid, pnc=pid)], dma_engine_mask=sum(1 << e for e in eng[q]),
+                                         remote_sem=S[sem], src=src(q), dst=dst(q)))
+        g.remote_dma_fused(trs, local_sem=S["ls"])
+
+    runs = {early: [(0, 0, C)], late: [(0, H, C)], near: [(0, 0, H), (H, 3 * H, H)]}
+    for a in (early, near, late):
+        h = 0 if a == early else 1
+        lq, lp, b = T["re%d" % h], T["rse%d" % h], a * C
+        g.wait_ge(S["qx%d" % a], 1)
+        for u, v, n in runs[a]:
+            fire([a], hop1, "ax%d" % r, lambda q: T.qx[:, b + u:b + u + n].bitcast(dt.uint8),
+                 lambda q: lq[:, v:v + n].bitcast(dt.uint8))
+        for u, v, n in runs[a]:
+            fire([a], hop1, "ax%d" % r, lambda q: T.sx[:, b + u:b + u + n], lambda q: lp[:, v:v + n])
+
+    def landed(s):
+        n = 4 if s == near else 2
+        P.wait_ge(S["ax%d" % s], n * len(roles(T, topo, s)[2][r]))
+
+    ts, tt = V.tensor_scalar, V.tensor_tensor
+    todo = [
+        (ts, (T.kf[:], T.plr[:], -0.5 * (TR - 1), 1.0 / TR, M.add, M.mult), ()),
+        (V.tensor_copy, (T.t0[:], T.kf[:]), (0,)),
+        (ts, (T.t1[:], T.t0[:], 3, None, M.arith_shift_right), (1,)),
+        (ts, (T.t2[:], T.t0[:], 2, 1, M.arith_shift_right, M.bitwise_and), (1,)),
+        (ts, (T.t3[:], T.t0[:], 1, None, M.bitwise_and), (1,)),
+        (ts, (T.t5[:], T.t0[:], 40.0, 80.0, M.mult, M.add), (1,)),
+        (tt, (T.t4[:], T.t2[:], T.t3[:], M.mult), (3, 4)),
+        (ts, (T.t6[:], T.t1[:], -600.0, None, M.mult), (2,)),
+        (ts, (T.t8[:], T.t3[:], 160.0, None, M.mult), (4,)),
+        (tt, (T.t9[:], T.plr[:], T.t5[:], M.add), (5,)),
+        (ts, (T.t7[:], T.t4[:], -640.0, None, M.mult), (6,)),
+        (tt, (T.t10[:], T.t6[:], T.t8[:], M.add), (7, 8)),
+        (tt, (T.t11[:], T.t10[:], T.t7[:], M.add), (10, 11)),
+        (tt, (T.t12[:], T.t9[:], T.t11[:], M.add), (9, 12)),
+        (V.tensor_copy, (T.poff[:], T.t12[:]), (13,)),
+    ]
+    done = [0]
+
+    def places(n):
+        for _ in range(n):
+            call, args, need = todo[done[0]]
+            if done[0] == 0:
+                V.wait_ge(S["pl"], 128)
+            for k in need:
+                V.wait_ge(S["k%d" % k], 1)
+            call(*args).then_inc(S["k%d" % done[0]], 1)
+            done[0] += 1
+
+    def product(k, cod, pla, c0):
+        for i in range(4):
+            b = 4 * (k % 2) + i
+            if k >= 2:
+                P.wait_ge(S["r%d_%d" % (k - 2, i)], 1)
+            P.matmul_mx(T.ps[:, 512 * b:512 * b + C], T.wq[:, 128 * i:128 * i + 128], T.ws[:, 128 * i:128 * i + 128],
+                        cod[:, c0:c0 + C], pla[:, c0:c0 + C], True, True).then_inc(S["m%d_%d" % (k, i)], 1)
+
+    def relu(k, i, pieces, hh, sem):
+        b = 512 * (4 * (k % 2) + i)
+        e = V if i % 2 else A
+        e.wait_ge(S["m%d_%d" % (k, i)], 1)
+        for c0, n, s, b0, b1 in pieces:
+            src = T.ps[:, b + c0:b + c0 + n]
+            dst = hh[:, b0:b1, 4 * TR * (s // 2) + i:4 * TR * (s // 2 + 1):4]
+            if e is A:
+                c = A.activation(dst, src, Relu, scale=0.043)
+            else:
+                c = V.tensor_scalar(dst, src, 0.0, 0.043, M.max, M.mult)
+            c.then_inc(S[sem], 1)
+
+    ow = 0 if odd else H
+    at = 0 if odd else 2 * H
+    view = H if odd else 0
+
+    def onward_far(h):
+        hh, qf, sf, lf, lsf = (T["%s%d" % (n, h)] for n in ("h", "qf", "sf", "lf", "lsf"))
+        sem, fl = "ah%d_%d" % (h, r), H * (1 - odd)
+        V.quantize_mx(qf[:], sf[:], hh[:, f0:f0 + 2, :]).then_inc(S["qhf%d" % h], 1)
+        g.wait_ge(S["qhf%d" % h], 1)
+        fire(far, hop2, sem, lambda q: qf[:, H * (q % 2):H * (q % 2) + H].bitcast(dt.uint8),
+             lambda q: lf[:, fl:fl + H].bitcast(dt.uint8))
+        fire(far, hop2, sem, lambda q: sf[:, H * (q % 2):H * (q % 2) + H], lambda q: lsf[:, fl:fl + H])
+
+    def onward_near(h):
+        hh, qo, so = (T["%s%d" % (n, h)] for n in ("h", "qo", "so"))
+        sem = "ah%d_%d" % (h, r)
+        V.quantize_mx(qo[:, ow:ow + 2 * H], so[:, ow:ow + 2 * H], hh[:, o0:o0 + 2, :]).then_inc(S["qho%d" % h], 1)
+        g.wait_ge(S["qho%d" % h], 1)
+        fire([near], hop2, sem, lambda q: qo[:, at:at + H].bitcast(dt.uint8), lambda q: qo[:, at:at + H].bitcast(dt.uint8))
+        fire([near], hop2, sem, lambda q: so[:, at:at + H], lambda q: so[:, at:at + H])
+
+    P.wait_ge(S["qw"], 1)
+    P.wait_ge(S["qx%d" % r], 1)
+    product(0, T.qx, T.sx, r * C)
+    landed(early)
+    product(1, T.re0, T.rse0, 0)
+    landed(near)
+    landed(late)
+    product(2, T.re1, T.rse1, f0 // 2 * C)
+    product(3, T.re1, T.rse1, o0 // 2 * C)
+
+    for k, s in ((0, r), (1, early)):
+        for i in range(4):
+            relu(k, i, [(0, C, s, 0, N)], T.h0, "r%d_%d" % (k, i))
+            if i % 2:
+                places(2)
+    for k in range(2):
+        for i in range(4):
+            V.wait_ge(S["r%d_%d" % (k, i)], 1)
+    onward_far(0)
+    onward_near(0)
+
+    def half1(k, p, sem):
+        for i in range(4):
+            two = (near, late) if p == 0 else (late, near)
+            relu(k, i, [(H * j, H, s, p, p + 2) for j, s in enumerate(two)], T.h1, sem)
+        V.wait_ge(S[sem], 8)
+
+    half1(2, f0, "rf")
+    onward_far(1)
+    half1(3, o0, "rn")
+    onward_near(1)
+    places(len(todo) - done[0])
+
+    P.wait_ge(S["qv"], 1)
+    for h in range(2):
+        P.wait_ge(S["qho%d" % h], 1)
+    for k in range(4):
+        h, out = k // 2, k % 2
+        if out:
+            cod, pla, c0, base = T["lf%d" % h], T["lsf%d" % h], 0, f0
+        else:
+            cod, pla, c0, base = T["qo%d" % h], T["so%d" % h], view, o0
+        for a in (far if out else [near]):
+            P.wait_ge(S["ah%d_%d" % (h, a)], 2 * len(roles(T, topo, a)[3][r]))
+        P.matmul_mx(T.ps[:, 512 * k:512 * k + C], T.vq[:], T.vs[:],
+                    cod[:, c0:c0 + C], pla[:, c0:c0 + C], True, True).then_inc(S["y%d" % k], 1)
+        p = 2 * C * h + C * (base // 2)
+        src, dst = T.ps[:, 512 * k:512 * k + C], T.ysb[:, p:p + C]
+        e = V if k == 3 else A
+        e.wait_ge(S["y%d" % k], 1)
+        (V.tensor_copy(dst, src) if e is V else A.activation(dst, src, Copy)).then_inc(S["c%d" % k], 1)
+    for e in (V, A):
+        e.wait_ge(S["k14"], 1)
+        for k in range(N):
+            e.wait_ge(S["c%d" % k], 1)
+    for j in range(2):
+        a = 256 * j
+        V.tensor_copy(T.yo[:, a:a + 128], T.ysb[:].indirect(T.poff[:, a // 16:a // 16 + 8])).then_inc(S["yd%d" % j], 1)
+        A.activation(T.yo[:, a + 128:a + 256], T.ysb[:].indirect(T.poff[:, a // 16 + 8:a // 16 + 16]), Copy).then_inc(S["yd%d" % j], 1)
+        g.sync.wait_ge(S["yd%d" % j], 2)
+        g.sync.dma_start(T.y[:, a:a + 256], T.yo[:, a:a + 256]).then_inc(S["st"], 16)
+    g.sync.wait_ge(S["st"], 32)
+    g.wait_ge(S["ls"], 2 * sum(len(hop1[q]) * len(runs[q]) for q in hop1) + 4 * sum(len(e) for e in hop2.values()))

@@ -4,270 +4,254 @@ from concourse.mybir import dt, AluOpType, ActivationFunctionType
 N, TR = 4, 40
 C = N * TR
 H = 2 * TR
+R = 3 * H
 W = N * C
 L = C // 16
 F8 = "float8_e4m3fn_x4"
-SCRATCH = {
-    "xb": ("sbuf", [128, 2048], "bfloat16"),
-    "wb": ("sbuf", [128, 2048], "bfloat16"),
-    "vb": ("sbuf", [128, 512], "bfloat16"),
-    "trl": ("sbuf", [128, 40], "int32"),
-    "plr": ("sbuf", [128, 32], "int32"),
-    "toff": ("sbuf", [128, 40], "uint16"),
-    "poff": ("sbuf", [128, 32], "uint16"),
-    "kf": ("sbuf", [128, 32], "float32"),
-    "xg": ("sbuf", [128, 4 * W], "bfloat16"),
-    "qx": ("sbuf", [128, W], F8),
-    "sx": ("sbuf", [128, W], "uint8"),
-    "re0": ("sbuf", [128, C], F8),
-    "rse0": ("sbuf", [128, C], "uint8"),
-    "re1": ("sbuf", [128, 2 * C], F8),
-    "rse1": ("sbuf", [128, 2 * C], "uint8"),
-    "wq": ("sbuf", [128, 512], F8),
-    "ws": ("sbuf", [128, 512], "uint8"),
-    "vq": ("sbuf", [128, 128], F8),
-    "vs": ("sbuf", [128, 128], "uint8"),
-    "ps": ("psum", [128, 4096], "float32"),
-    "ysb": ("sbuf", [128, W], "float32"),
-    "yo": ("sbuf", [128, 512], "float32"),
+
+CFG = {
+    "A": "e2 e3 n2 n3 l2 l3 o1 o2 o3 oA0 oA2 nA0 nA2 eA0 eA1 eA2 lF0 lF2 lL0 lL2 lL3",
+    "V": "e0 e1 n0 pe n1 l0 pn l1 o0 pl w po v k0 oA1 oA3 nA1 nA3 k1 X0 eA3 k2 lF1 lF3 lL1 Y X1 N O k3 k4",
+    "G": "e n l X0 Y:q X1:q N:q YN:s X1:s",
+    "prods": "onel",
+    "last": "X0A OA NA YV X1A",
+    "x": "e",
 }
-for _h in range(2):
-    SCRATCH.update({
-        "h%d" % _h: ("sbuf", [128, N, 4 * H], "bfloat16"),
-        "qf%d" % _h: ("sbuf", [128, 2 * H], F8),
-        "sf%d" % _h: ("sbuf", [128, 2 * H], "uint8"),
-        "qo%d" % _h: ("sbuf", [128, 3 * H], F8),
-        "so%d" % _h: ("sbuf", [128, 3 * H], "uint8"),
-        "lf%d" % _h: ("sbuf", [128, 2 * H], F8),
-        "lsf%d" % _h: ("sbuf", [128, 2 * H], "uint8"),
-    })
-for _j in range(13):
-    SCRATCH["t%d" % _j] = ("sbuf", [128, 32], "int32")
-SEMAPHORES = (["tl", "xl", "wl", "vl", "pl", "tof", "qw", "qv", "rf", "rn", "ls", "yd0", "yd1", "st"]
-              + ["g%d" % j for j in range(N)] + ["qx%d" % j for j in range(N)]
-              + ["qhf%d" % j for j in range(2)] + ["qho%d" % j for j in range(2)]
-              + ["k%d" % j for j in range(15)]
-              + ["m%d_%d" % (k, i) for k in range(N) for i in range(4)]
-              + ["r%d_%d" % (k, i) for k in range(2) for i in range(4)]
-              + ["ax%d" % j for j in range(N)] + ["ah%d_%d" % (h, j) for h in range(2) for j in range(N)]
-              + ["y%d" % j for j in range(N)] + ["c%d" % j for j in range(N)])
 
 
-def roles(T, topo, r):
-    me = T.cores[r]
-    far = [q for q in range(N) if topo.chip(T.cores[q]) != topo.chip(me)]
-    far.sort(key=lambda q: (q % 2 != r % 2, q))
-    near = [q for q in range(N) if q != r and q not in far][0]
-    out = topo.engines(me, T.cores[far[0]])
-    half = len(out) // 2
-    inside = [e for e in topo.engines(me, T.cores[near]) if e not in out]
-    hop1 = {far[0]: out, far[1]: out, near: inside}
-    hop2 = {far[0]: out[:half], far[1]: out[half:], near: inside}
-    return far, near, hop1, hop2
+def scratch(cfg):
+    d = {
+        "xb": ("sbuf", [128, 2048], "bfloat16"),
+        "wb": ("sbuf", [128, 2048], "bfloat16"),
+        "vb": ("sbuf", [128, 512], "bfloat16"),
+        "trl": ("sbuf", [128, N * L], "int32"),
+        "plr": ("sbuf", [128, 32], "int32"),
+        "toff": ("sbuf", [128, N * L], "uint16"),
+        "poff": ("sbuf", [128, 32], "uint16"),
+        "xg": ("sbuf", [128, 4 * W], "bfloat16"),
+        "ps": ("psum", [128, 4096], "float32"),
+        "ysb": ("sbuf", [128, W], "float32"),
+        "yo": ("sbuf", [128, 512], "float32"),
+        "h": ("sbuf", [128, N, 2 * 192 + 4 * C], "bfloat16"),
+    }
+    for n, c in (("w", 512), ("v", 128), ("x", W), ("lx", W), ("X0", 128), ("X1", 128), ("Y", C), ("N", C), ("O", C + H),
+                 ("lF", C + H), ("lN", C)):
+        d["q" + n] = ("sbuf", [128, c], F8)
+        d["s" + n] = ("sbuf", [128, c], "uint8")
+    for j in range(5):
+        d["t%d" % j] = ("sbuf", [128, 32], "int32")
+    return d
+
+
+SCRATCH = scratch(CFG)
+SEMAPHORES = (["tl", "xl", "wl", "vl", "pl", "tof", "pw", "pv", "ls", "yd0", "yd1", "st", "cp", "z"]
+              + ["g" + c for c in "oenl"] + ["px" + c for c in "oenl"] + ["ax%d" % j for j in range(N)]
+              + [a + k for a in "pa" for k in ("X0", "X1", "Y", "N", "O")]
+              + ["k%d" % j for j in range(4)]
+              + ["m%d_%d" % (k, i) for k in range(N + 1) for i in range(4)]
+              + ["r%s%d_%d" % (p, k, i) for p in "FL" for k in range(N) for i in range(4)]
+              + ["y%d" % j for j in range(6)])
+
+
+def role(a, c):
+    return a ^ "onel".index(c)
 
 
 def rank_program(g, core, T, topo):
     r = T.rank_of(core)
     if r is None:
         return
+    cfg = CFG
     S = T.sem
     V, A, P = g.vector, g.scalar, g.tensor
     Copy, Relu, M = ActivationFunctionType.Copy, ActivationFunctionType.Relu, AluOpType
-    far, near, hop1, hop2 = roles(T, topo, r)
-    early, late = far
-    f0, o0 = 2 * (far[0] // 2), 2 * (r // 2)
-    assert sorted(far) == [f0, f0 + 1] and sorted([r, near]) == [o0, o0 + 1]
-    odd = r % 2
+    far = [q for q in range(N) if topo.chip(T.cores[q]) != topo.chip(core)]
+    near = role(r, "n")
+    f0, o0 = min(far), min(r, near)
+    assert far == [f0, f0 + 1] == sorted((role(r, "e"), role(r, "l"))) and f0 % 2 == 0 and o0 % 2 == 0
+    out = topo.engines(core, T.cores[f0])
+    inside = [e for e in topo.engines(core, T.cores[near]) if e not in out]
+    eng = {f0: out, f0 + 1: out, near: inside}
+    prods = cfg["prods"]
+    calls = (cfg["A"] + " " + cfg["V"]).split()
+    fx = role(r, cfg["x"])
+    fy = 2 * f0 + 1 - fx
+    Z = 192
 
-    for k in range(8):
-        q = g.sync if k < 4 else A
+    for k, q in enumerate((g.sync, A)):
         q.dma_start(T.trl[16 * k:16 * k + 16, :], T.tri[:]).then_inc(S["tl"], 16)
     g.sync.dma_start(T.xb[:], T.x[:]).then_inc(S["xl"], 16)
     g.sync.dma_start(T.wb[:], T.w[:]).then_inc(S["wl"], 16)
     g.sync.dma_start(T.vb[:], T.vv[:]).then_inc(S["vl"], 16)
-    for k in range(8):
-        g.sync.dma_start(T.plr[16 * k:16 * k + 16, :], T.plt[:]).then_inc(S["pl"], 16)
+    for k in range(2):
+        A.dma_start(T.plr[16 * k:16 * k + 16, :], T.plt[:]).then_inc(S["pl"], 16)
 
-    V.wait_ge(S["tl"], 128)
-    V.tensor_scalar(T.toff[:], T.trl[:], 0.0, 4.0, M.max, M.mult).then_inc(S["tof"], 1)
+    V.memset(T.h[:, fx, 0:Z], 0.0).then_inc(S["z"], 1)
+    V.memset(T.h[:, fx, Z + 4 * C:2 * Z + 4 * C], 0.0).then_inc(S["z"], 1)
+    V.wait_ge(S["tl"], 32)
+    for k in range(4):
+        V.tensor_scalar(T.toff[32 * k:32 * k + 32, :], T.trl[0:32, :], 0.0, 4.0, M.max, M.mult).then_inc(S["tof"], 1)
+    V.wait_ge(S["z"], 2)
     for e in (V, A):
-        e.wait_ge(S["tof"], 1)
+        e.wait_ge(S["tof"], 4)
         e.wait_ge(S["xl"], 16)
 
-    def gather(a, nv):
-        for t in range(4):
-            src = T.xb[:, t:2048].indirect(T.toff[:, a * L:(a + 1) * L])
-            dst = T.xg[:, a * 4 * C + t:(a + 1) * 4 * C:4]
-            if t < nv:
-                V.tensor_copy(dst, src).then_inc(S["g%d" % a], 1)
-            else:
-                A.activation(dst, src, Copy).then_inc(S["g%d" % a], 1)
+    def gather(e, c, t):
+        a = role(r, c)
+        src = T.xb[:, t:2048].indirect(T.toff[:, a * L:a * L + L])
+        dst = T.xg[:, a * 4 * C + t:(a + 1) * 4 * C:4]
+        (V.tensor_copy(dst, src) if e is V else A.activation(dst, src, Copy)).then_inc(S["g" + c], 1)
 
-    def pack(a):
-        V.wait_ge(S["g%d" % a], 4)
-        V.quantize_mx(T.qx[:, a * C:(a + 1) * C], T.sx[:, a * C:(a + 1) * C],
-                      T.xg[:, a * 4 * C:(a + 1) * 4 * C]).then_inc(S["qx%d" % a], 1)
+    def pack(c):
+        a = role(r, c)
+        V.wait_ge(S["g" + c], 4)
+        V.quantize_mx(T.qx[:, a * C:a * C + C], T.sx[:, a * C:a * C + C], T.xg[:, a * 4 * C:(a + 1) * 4 * C]).then_inc(S["px" + c], 1)
 
-    for a, nv in ((early, 2), (near, 2), (late, 1)):
-        gather(a, nv)
-        pack(a)
-    gather(r, 1)
-    V.wait_ge(S["wl"], 16)
-    V.quantize_mx(T.wq[:], T.ws[:], T.wb[:]).then_inc(S["qw"], 1)
-    pack(r)
-    V.wait_ge(S["vl"], 16)
-    V.quantize_mx(T.vq[:], T.vs[:], T.vb[:]).then_inc(S["qv"], 1)
+    def done(c, kind, i):
+        return "r%s%d_%d" % ("F" if c + "A0" in calls else kind, prods.index(c), i)
 
-    def fire(qs, eng, sem, src, dst):
-        trs = []
-        for q in qs:
-            rid, pid = topo.addr(T.cores[q])[:2]
-            trs.append(RemoteDMATransfer(dst_ids=[DstId(rid=rid, pnc=pid)], dma_engine_mask=sum(1 << e for e in eng[q]),
-                                         remote_sem=S[sem], src=src(q), dst=dst(q)))
-        g.remote_dma_fused(trs, local_sem=S["ls"])
+    def window(q0):
+        return C - 128 if q0 else 0
 
-    runs = {early: [(0, 0, C)], late: [(0, H, C)], near: [(0, 0, H), (H, 3 * H, H)]}
-    for a in (early, near, late):
-        h = 0 if a == early else 1
-        lq, lp, b = T["re%d" % h], T["rse%d" % h], a * C
-        g.wait_ge(S["qx%d" % a], 1)
-        for u, v, n in runs[a]:
-            fire([a], hop1, "ax%d" % r, lambda q: T.qx[:, b + u:b + u + n].bitcast(dt.uint8),
-                 lambda q: lq[:, v:v + n].bitcast(dt.uint8))
-        for u, v, n in runs[a]:
-            fire([a], hop1, "ax%d" % r, lambda q: T.sx[:, b + u:b + u + n], lambda q: lp[:, v:v + n])
+    narrow = prods[3] + "A0" not in calls
 
-    def landed(s):
-        n = 4 if s == near else 2
-        P.wait_ge(S["ax%d" % s], n * len(roles(T, topo, s)[2][r]))
-
-    ts, tt = V.tensor_scalar, V.tensor_tensor
-    todo = [
-        (ts, (T.kf[:], T.plr[:], -0.5 * (TR - 1), 1.0 / TR, M.add, M.mult), ()),
-        (V.tensor_copy, (T.t0[:], T.kf[:]), (0,)),
-        (ts, (T.t1[:], T.t0[:], 3, None, M.arith_shift_right), (1,)),
-        (ts, (T.t2[:], T.t0[:], 2, 1, M.arith_shift_right, M.bitwise_and), (1,)),
-        (ts, (T.t3[:], T.t0[:], 1, None, M.bitwise_and), (1,)),
-        (ts, (T.t5[:], T.t0[:], 40.0, 80.0, M.mult, M.add), (1,)),
-        (tt, (T.t4[:], T.t2[:], T.t3[:], M.mult), (3, 4)),
-        (ts, (T.t6[:], T.t1[:], -600.0, None, M.mult), (2,)),
-        (ts, (T.t8[:], T.t3[:], 160.0, None, M.mult), (4,)),
-        (tt, (T.t9[:], T.plr[:], T.t5[:], M.add), (5,)),
-        (ts, (T.t7[:], T.t4[:], -640.0, None, M.mult), (6,)),
-        (tt, (T.t10[:], T.t6[:], T.t8[:], M.add), (7, 8)),
-        (tt, (T.t11[:], T.t10[:], T.t7[:], M.add), (10, 11)),
-        (tt, (T.t12[:], T.t9[:], T.t11[:], M.add), (9, 12)),
-        (V.tensor_copy, (T.poff[:], T.t12[:]), (13,)),
-    ]
-    done = [0]
-
-    def places(n):
-        for _ in range(n):
-            call, args, need = todo[done[0]]
-            if done[0] == 0:
-                V.wait_ge(S["pl"], 128)
-            for k in need:
-                V.wait_ge(S["k%d" % k], 1)
-            call(*args).then_inc(S["k%d" % done[0]], 1)
-            done[0] += 1
-
-    def product(k, cod, pla, c0):
+    def product(k):
+        c = prods[min(k, 3)]
+        s = role(r, c)
+        if s == r:
+            P.wait_ge(S["pxo"], 1)
+        elif k < N:
+            P.wait_ge(S["ax%d" % s], 2 * len(eng[s]))
+        cod, pla = (T.qx, T.sx) if s == r else (T.qlx, T.slx)
+        u, n = (s * C, C) if k < 3 or not narrow else (s * C + window(f0 if k == 3 else o0), 128)
         for i in range(4):
-            b = 4 * (k % 2) + i
+            b = 512 * (4 * (k % 2) + i)
             if k >= 2:
-                P.wait_ge(S["r%d_%d" % (k - 2, i)], 1)
-            P.matmul_mx(T.ps[:, 512 * b:512 * b + C], T.wq[:, 128 * i:128 * i + 128], T.ws[:, 128 * i:128 * i + 128],
-                        cod[:, c0:c0 + C], pla[:, c0:c0 + C], True, True).then_inc(S["m%d_%d" % (k, i)], 1)
+                for sem in sorted({done(prods[k - 2], p, i) for p in "FL"}):
+                    P.wait_ge(S[sem], 1)
+            P.matmul_mx(T.ps[:, b:b + n], T.qw[:, 128 * i:128 * i + 128], T.sw[:, 128 * i:128 * i + 128],
+                        cod[:, u:u + n], pla[:, u:u + n], True, True).then_inc(S["m%d_%d" % (k, i)], 1)
 
-    def relu(k, i, pieces, hh, sem):
-        b = 512 * (4 * (k % 2) + i)
-        e = V if i % 2 else A
+    def relu(e, c, kind, i):
+        k, s = prods.index(c), role(r, c)
+        q0, q1 = {"F": (f0, f0 + 2), "L": (o0, o0 + 2), "A": (0, N)}[kind]
+        skip = 0
+        if k == 3 and narrow:
+            skip, k = window(q0), (3 if kind == "F" else 4)
+        b = 512 * (4 * (k % 2) + i) - skip
         e.wait_ge(S["m%d_%d" % (k, i)], 1)
-        for c0, n, s, b0, b1 in pieces:
-            src = T.ps[:, b + c0:b + c0 + n]
-            dst = hh[:, b0:b1, 4 * TR * (s // 2) + i:4 * TR * (s // 2 + 1):4]
-            if e is A:
-                c = A.activation(dst, src, Relu, scale=0.043)
-            else:
-                c = V.tensor_scalar(dst, src, 0.0, 0.043, M.max, M.mult)
-            c.then_inc(S[sem], 1)
-
-    ow = 0 if odd else H
-    at = 0 if odd else 2 * H
-    view = H if odd else 0
-
-    def onward_far(h):
-        hh, qf, sf, lf, lsf = (T["%s%d" % (n, h)] for n in ("h", "qf", "sf", "lf", "lsf"))
-        sem, fl = "ah%d_%d" % (h, r), H * (1 - odd)
-        V.quantize_mx(qf[:], sf[:], hh[:, f0:f0 + 2, :]).then_inc(S["qhf%d" % h], 1)
-        g.wait_ge(S["qhf%d" % h], 1)
-        fire(far, hop2, sem, lambda q: qf[:, H * (q % 2):H * (q % 2) + H].bitcast(dt.uint8),
-             lambda q: lf[:, fl:fl + H].bitcast(dt.uint8))
-        fire(far, hop2, sem, lambda q: sf[:, H * (q % 2):H * (q % 2) + H], lambda q: lsf[:, fl:fl + H])
-
-    def onward_near(h):
-        hh, qo, so = (T["%s%d" % (n, h)] for n in ("h", "qo", "so"))
-        sem = "ah%d_%d" % (h, r)
-        V.quantize_mx(qo[:, ow:ow + 2 * H], so[:, ow:ow + 2 * H], hh[:, o0:o0 + 2, :]).then_inc(S["qho%d" % h], 1)
-        g.wait_ge(S["qho%d" % h], 1)
-        fire([near], hop2, sem, lambda q: qo[:, at:at + H].bitcast(dt.uint8), lambda q: qo[:, at:at + H].bitcast(dt.uint8))
-        fire([near], hop2, sem, lambda q: so[:, at:at + H], lambda q: so[:, at:at + H])
-
-    P.wait_ge(S["qw"], 1)
-    P.wait_ge(S["qx%d" % r], 1)
-    product(0, T.qx, T.sx, r * C)
-    landed(early)
-    product(1, T.re0, T.rse0, 0)
-    landed(near)
-    landed(late)
-    product(2, T.re1, T.rse1, f0 // 2 * C)
-    product(3, T.re1, T.rse1, o0 // 2 * C)
-
-    for k, s in ((0, r), (1, early)):
-        for i in range(4):
-            relu(k, i, [(0, C, s, 0, N)], T.h0, "r%d_%d" % (k, i))
-            if i % 2:
-                places(2)
-    for k in range(2):
-        for i in range(4):
-            V.wait_ge(S["r%d_%d" % (k, i)], 1)
-    onward_far(0)
-    onward_near(0)
-
-    def half1(k, p, sem):
-        for i in range(4):
-            two = (near, late) if p == 0 else (late, near)
-            relu(k, i, [(H * j, H, s, p, p + 2) for j, s in enumerate(two)], T.h1, sem)
-        V.wait_ge(S[sem], 8)
-
-    half1(2, f0, "rf")
-    onward_far(1)
-    half1(3, o0, "rn")
-    onward_near(1)
-    places(len(todo) - done[0])
-
-    P.wait_ge(S["qv"], 1)
-    for h in range(2):
-        P.wait_ge(S["qho%d" % h], 1)
-    for k in range(4):
-        h, out = k // 2, k % 2
-        if out:
-            cod, pla, c0, base = T["lf%d" % h], T["lsf%d" % h], 0, f0
+        src, dst = T.ps[:, b + TR * q0:b + TR * q1], T.h[:, q0:q1, Z + 4 * TR * s + i:Z + 4 * TR * (s + 1):4]
+        if e is A:
+            call = A.activation(dst, src, Relu, scale=0.043)
         else:
-            cod, pla, c0, base = T["qo%d" % h], T["so%d" % h], view, o0
-        for a in (far if out else [near]):
-            P.wait_ge(S["ah%d_%d" % (h, a)], 2 * len(roles(T, topo, a)[3][r]))
-        P.matmul_mx(T.ps[:, 512 * k:512 * k + C], T.vq[:], T.vs[:],
-                    cod[:, c0:c0 + C], pla[:, c0:c0 + C], True, True).then_inc(S["y%d" % k], 1)
-        p = 2 * C * h + C * (base // 2)
-        src, dst = T.ps[:, 512 * k:512 * k + C], T.ysb[:, p:p + C]
-        e = V if k == 3 else A
+            call = V.tensor_scalar(dst, src, 0.0, 0.043, M.max, M.mult)
+        call.then_inc(S[done(c, kind, i)], 1)
+
+    def half(first):
+        return (0, 128, 128 - H, H) if first == 0 else (Z + 4 * H, 128, 0, H)
+
+    message = {"X0": (fx, "on") + half(o0), "X1": (fx, "el") + half(f0),
+               "Y": (fy, "onel", Z, C, 0, C), "N": (near, "onel", Z, C, 0, C), "O": (r, "onel", Z, C, 0, C)}
+    waited = set()
+
+    def repack(name):
+        b, roles, u, n = message[name][:4]
+        for sem in sorted({done(c, "F" if b in far else "L", i) for c in roles for i in range(4)} - waited):
+            V.wait_ge(S[sem], 1)
+            waited.add(sem)
+        V.quantize_mx(T["q" + name][:, 0:n], T["s" + name][:, 0:n], T.h[:, b, u:u + 4 * n]).then_inc(S["p" + name], 1)
+
+    pl, t0, t1, t2, t3, t4 = (t[0:32, :] for t in (T.plr, T.t0, T.t1, T.t2, T.t3, T.t4))
+
+    def places(k):
+        if k == 0:
+            V.wait_ge(S["pl"], 32)
+            V.tensor_scalar(t0, pl, -0.5 * (TR - 1), 1.0 / TR, M.add, M.mult).then_inc(S["k0"], 1)
+            V.tensor_scalar(t1, pl, -0.5 * (C - 1), 1.0 / C, M.add, M.mult).then_inc(S["k0"], 1)
+        elif k == 1:
+            V.wait_ge(S["k0"], 2)
+            V.tensor_scalar(t2, t0, 1.0 * (C - TR), None, M.mult).then_inc(S["k1"], 1)
+            V.tensor_scalar(t4, t1, TR - 1.0 * W, None, M.mult).then_inc(S["k1"], 1)
+        elif k == 2:
+            V.wait_ge(S["k1"], 2)
+            V.tensor_tensor(t3, t4, t2, M.add).then_inc(S["k1"], 1)
+        elif k == 3:
+            V.wait_ge(S["k1"], 3)
+            V.tensor_tensor(t0, pl, t3, M.add).then_inc(S["k2"], 1)
+        else:
+            V.wait_ge(S["k2"], 1)
+            for u in range(4):
+                V.tensor_copy(T.poff[32 * u:32 * u + 32, :], t0).then_inc(S["k3"], 1)
+
+    for e, name in ((A, "A"), (V, "V")):
+        for step in cfg[name].split():
+            if step == "w":
+                V.wait_ge(S["wl"], 16)
+                V.quantize_mx(T.qw[:], T.sw[:], T.wb[:]).then_inc(S["pw"], 1)
+            elif step == "v":
+                V.wait_ge(S["vl"], 16)
+                V.quantize_mx(T.qv[:], T.sv[:], T.vb[:]).then_inc(S["pv"], 1)
+            elif step[0] == "p":
+                pack(step[1])
+            elif step[0] == "k":
+                places(int(step[1]))
+            elif step in message:
+                repack(step)
+            elif len(step) == 3:
+                relu(e, step[0], step[1], int(step[2]))
+            else:
+                gather(e, step[0], int(step[1]))
+    P.wait_ge(S["pw"], 1)
+    for k in range(N + narrow):
+        product(k)
+
+    lands = {"X0": ("O", C), "X1": ("lF", C), "Y": ("lF", 0), "N": ("lN", 0), "O": ("O", 0)}
+    sent = 0
+    for step in cfg["G"].split():
+        step, kinds = (step + ":qs").split(":")[:2]
+        parts = []
+        for name in ([step] if step in message else step):
+            if name in "enl":
+                a = role(r, name)
+                g.wait_ge(S["px" + name], 1)
+                parts.append((a, "ax%d" % r, "x", a * C, "lx", r * C, C))
+            else:
+                g.wait_ge(S["p" + name], 1)
+                parts.append((message[name][0], "a" + name, name, message[name][4]) + lands[name] + (message[name][5],))
+        for kind in kinds:
+            trs = []
+            for q, sem, src, c0, dst, at, n in parts:
+                rid, pid = topo.addr(T.cores[q])[:2]
+                u, v = T[kind + src][:, c0:c0 + n], T[kind + dst][:, at:at + n]
+                if kind == "q":
+                    u, v = u.bitcast(dt.uint8), v.bitcast(dt.uint8)
+                trs.append(RemoteDMATransfer(dst_ids=[DstId(rid=rid, pnc=pid)], dma_engine_mask=sum(1 << e for e in eng[q]),
+                                             remote_sem=S[sem], src=u, dst=v))
+                sent += len(eng[q])
+            g.remote_dma_fused(trs, local_sem=S["ls"])
+
+    P.wait_ge(S["pv"], 1)
+    for name in message:
+        P.wait_ge(S["p" + name], 1)
+    last = cfg["last"].split()
+    goes = {"X0": fx * C + f0 * TR, "X1": fx * C + o0 * TR, "Y": fy * C, "N": near * C, "O": r * C}
+    seen = {"O"}
+    for k, step in enumerate(last):
+        name, e = step[:-1], (V if step[-1] == "V" else A)
+        (buf, c0), n = lands[name], message[name][5]
+        lead = max(0, 128 - n)
+        for u in ([name, "Y"] if name == "X1" else [name]):
+            if u not in seen:
+                P.wait_ge(S["a" + u], 2 * len(out))
+                seen.add(u)
+        P.matmul_mx(T.ps[:, 512 * k:512 * k + lead + n], T.qv[:], T.sv[:], T["q" + buf][:, c0 - lead:c0 + n],
+                    T["s" + buf][:, c0 - lead:c0 + n], True, True).then_inc(S["y%d" % k], 1)
         e.wait_ge(S["y%d" % k], 1)
-        (V.tensor_copy(dst, src) if e is V else A.activation(dst, src, Copy)).then_inc(S["c%d" % k], 1)
+        src, dst = T.ps[:, 512 * k + lead:512 * k + lead + n], T.ysb[:, goes[name]:goes[name] + n]
+        (V.tensor_copy(dst, src) if e is V else A.activation(dst, src, Copy)).then_inc(S["cp"], 1)
     for e in (V, A):
-        e.wait_ge(S["k14"], 1)
-        for k in range(N):
-            e.wait_ge(S["c%d" % k], 1)
+        e.wait_ge(S["k3"], 4)
+        e.wait_ge(S["cp"], len(last))
     for j in range(2):
         a = 256 * j
         V.tensor_copy(T.yo[:, a:a + 128], T.ysb[:].indirect(T.poff[:, a // 16:a // 16 + 8])).then_inc(S["yd%d" % j], 1)
@@ -275,4 +259,4 @@ def rank_program(g, core, T, topo):
         g.sync.wait_ge(S["yd%d" % j], 2)
         g.sync.dma_start(T.y[:, a:a + 256], T.yo[:, a:a + 256]).then_inc(S["st"], 16)
     g.sync.wait_ge(S["st"], 32)
-    g.wait_ge(S["ls"], 2 * sum(len(hop1[q]) * len(runs[q]) for q in hop1) + 4 * sum(len(e) for e in hop2.values()))
+    g.wait_ge(S["ls"], sent)

from concourse.bass import DstId, RemoteDMATransfer
from concourse.mybir import dt, AluOpType, ActivationFunctionType

N, TR = 4, 40
C = N * TR
H = 2 * TR
R = 3 * H
W = N * C
L = C // 16
F8 = "float8_e4m3fn_x4"

CFG = {
    "A": "e2 e3 n2 n3 l2 l3 o1 o2 o3 oA0 oA2 nA0 nA2 eA0 eA1 eA2 lF0 lF2 lL0 lL2 lL3",
    "V": "e0 e1 n0 pe n1 l0 pn l1 o0 pl w po v k0 oA1 oA3 nA1 nA3 k1 X0 eA3 k2 lF1 lF3 lL1 Y X1 N O k3 k4",
    "G": "e n l X0 Y:q X1:q N:q YN:s X1:s",
    "prods": "onel",
    "last": "X0A OA NA YV X1A",
    "x": "e",
}


def scratch(cfg):
    d = {
        "xb": ("sbuf", [128, 2048], "bfloat16"),
        "wb": ("sbuf", [128, 2048], "bfloat16"),
        "vb": ("sbuf", [128, 512], "bfloat16"),
        "trl": ("sbuf", [128, N * L], "int32"),
        "plr": ("sbuf", [128, 32], "int32"),
        "toff": ("sbuf", [128, N * L], "uint16"),
        "poff": ("sbuf", [128, 32], "uint16"),
        "xg": ("sbuf", [128, 4 * W], "bfloat16"),
        "ps": ("psum", [128, 4096], "float32"),
        "ysb": ("sbuf", [128, W], "float32"),
        "yo": ("sbuf", [128, 512], "float32"),
        "h": ("sbuf", [128, N, 2 * 192 + 4 * C], "bfloat16"),
    }
    for n, c in (("w", 512), ("v", 128), ("x", W), ("lx", W), ("X0", 128), ("X1", 128), ("Y", C), ("N", C), ("O", C + H),
                 ("lF", C + H), ("lN", C)):
        d["q" + n] = ("sbuf", [128, c], F8)
        d["s" + n] = ("sbuf", [128, c], "uint8")
    for j in range(5):
        d["t%d" % j] = ("sbuf", [128, 32], "int32")
    return d


SCRATCH = scratch(CFG)
SEMAPHORES = (["tl", "xl", "wl", "vl", "pl", "tof", "pw", "pv", "ls", "yd0", "yd1", "st", "cp", "z"]
              + ["g" + c for c in "oenl"] + ["px" + c for c in "oenl"] + ["ax%d" % j for j in range(N)]
              + [a + k for a in "pa" for k in ("X0", "X1", "Y", "N", "O")]
              + ["k%d" % j for j in range(4)]
              + ["m%d_%d" % (k, i) for k in range(N + 1) for i in range(4)]
              + ["r%s%d_%d" % (p, k, i) for p in "FL" for k in range(N) for i in range(4)]
              + ["y%d" % j for j in range(6)])


def role(a, c):
    return a ^ "onel".index(c)


def rank_program(g, core, T, topo):
    r = T.rank_of(core)
    if r is None:
        return
    cfg = CFG
    S = T.sem
    V, A, P = g.vector, g.scalar, g.tensor
    Copy, Relu, M = ActivationFunctionType.Copy, ActivationFunctionType.Relu, AluOpType
    far = [q for q in range(N) if topo.chip(T.cores[q]) != topo.chip(core)]
    near = role(r, "n")
    f0, o0 = min(far), min(r, near)
    assert far == [f0, f0 + 1] == sorted((role(r, "e"), role(r, "l"))) and f0 % 2 == 0 and o0 % 2 == 0
    out = topo.engines(core, T.cores[f0])
    inside = [e for e in topo.engines(core, T.cores[near]) if e not in out]
    eng = {f0: out, f0 + 1: out, near: inside}
    prods = cfg["prods"]
    calls = (cfg["A"] + " " + cfg["V"]).split()
    fx = role(r, cfg["x"])
    fy = 2 * f0 + 1 - fx
    Z = 192

    for k, q in enumerate((g.sync, A)):
        q.dma_start(T.trl[16 * k:16 * k + 16, :], T.tri[:]).then_inc(S["tl"], 16)
    g.sync.dma_start(T.xb[:], T.x[:]).then_inc(S["xl"], 16)
    g.sync.dma_start(T.wb[:], T.w[:]).then_inc(S["wl"], 16)
    g.sync.dma_start(T.vb[:], T.vv[:]).then_inc(S["vl"], 16)
    for k in range(2):
        A.dma_start(T.plr[16 * k:16 * k + 16, :], T.plt[:]).then_inc(S["pl"], 16)

    V.memset(T.h[:, fx, 0:Z], 0.0).then_inc(S["z"], 1)
    V.memset(T.h[:, fx, Z + 4 * C:2 * Z + 4 * C], 0.0).then_inc(S["z"], 1)
    V.wait_ge(S["tl"], 32)
    for k in range(4):
        V.tensor_scalar(T.toff[32 * k:32 * k + 32, :], T.trl[0:32, :], 0.0, 4.0, M.max, M.mult).then_inc(S["tof"], 1)
    V.wait_ge(S["z"], 2)
    for e in (V, A):
        e.wait_ge(S["tof"], 4)
        e.wait_ge(S["xl"], 16)

    def gather(e, c, t):
        a = role(r, c)
        src = T.xb[:, t:2048].indirect(T.toff[:, a * L:a * L + L])
        dst = T.xg[:, a * 4 * C + t:(a + 1) * 4 * C:4]
        (V.tensor_copy(dst, src) if e is V else A.activation(dst, src, Copy)).then_inc(S["g" + c], 1)

    def pack(c):
        a = role(r, c)
        V.wait_ge(S["g" + c], 4)
        V.quantize_mx(T.qx[:, a * C:a * C + C], T.sx[:, a * C:a * C + C], T.xg[:, a * 4 * C:(a + 1) * 4 * C]).then_inc(S["px" + c], 1)

    def done(c, kind, i):
        return "r%s%d_%d" % ("F" if c + "A0" in calls else kind, prods.index(c), i)

    def window(q0):
        return C - 128 if q0 else 0

    narrow = prods[3] + "A0" not in calls

    def product(k):
        c = prods[min(k, 3)]
        s = role(r, c)
        if s == r:
            P.wait_ge(S["pxo"], 1)
        elif k < N:
            P.wait_ge(S["ax%d" % s], 2 * len(eng[s]))
        cod, pla = (T.qx, T.sx) if s == r else (T.qlx, T.slx)
        u, n = (s * C, C) if k < 3 or not narrow else (s * C + window(f0 if k == 3 else o0), 128)
        for i in range(4):
            b = 512 * (4 * (k % 2) + i)
            if k >= 2:
                for sem in sorted({done(prods[k - 2], p, i) for p in "FL"}):
                    P.wait_ge(S[sem], 1)
            P.matmul_mx(T.ps[:, b:b + n], T.qw[:, 128 * i:128 * i + 128], T.sw[:, 128 * i:128 * i + 128],
                        cod[:, u:u + n], pla[:, u:u + n], True, True).then_inc(S["m%d_%d" % (k, i)], 1)

    def relu(e, c, kind, i):
        k, s = prods.index(c), role(r, c)
        q0, q1 = {"F": (f0, f0 + 2), "L": (o0, o0 + 2), "A": (0, N)}[kind]
        skip = 0
        if k == 3 and narrow:
            skip, k = window(q0), (3 if kind == "F" else 4)
        b = 512 * (4 * (k % 2) + i) - skip
        e.wait_ge(S["m%d_%d" % (k, i)], 1)
        src, dst = T.ps[:, b + TR * q0:b + TR * q1], T.h[:, q0:q1, Z + 4 * TR * s + i:Z + 4 * TR * (s + 1):4]
        if e is A:
            call = A.activation(dst, src, Relu, scale=0.043)
        else:
            call = V.tensor_scalar(dst, src, 0.0, 0.043, M.max, M.mult)
        call.then_inc(S[done(c, kind, i)], 1)

    def half(first):
        return (0, 128, 128 - H, H) if first == 0 else (Z + 4 * H, 128, 0, H)

    message = {"X0": (fx, "on") + half(o0), "X1": (fx, "el") + half(f0),
               "Y": (fy, "onel", Z, C, 0, C), "N": (near, "onel", Z, C, 0, C), "O": (r, "onel", Z, C, 0, C)}
    waited = set()

    def repack(name):
        b, roles, u, n = message[name][:4]
        for sem in sorted({done(c, "F" if b in far else "L", i) for c in roles for i in range(4)} - waited):
            V.wait_ge(S[sem], 1)
            waited.add(sem)
        V.quantize_mx(T["q" + name][:, 0:n], T["s" + name][:, 0:n], T.h[:, b, u:u + 4 * n]).then_inc(S["p" + name], 1)

    pl, t0, t1, t2, t3, t4 = (t[0:32, :] for t in (T.plr, T.t0, T.t1, T.t2, T.t3, T.t4))

    def places(k):
        if k == 0:
            V.wait_ge(S["pl"], 32)
            V.tensor_scalar(t0, pl, -0.5 * (TR - 1), 1.0 / TR, M.add, M.mult).then_inc(S["k0"], 1)
            V.tensor_scalar(t1, pl, -0.5 * (C - 1), 1.0 / C, M.add, M.mult).then_inc(S["k0"], 1)
        elif k == 1:
            V.wait_ge(S["k0"], 2)
            V.tensor_scalar(t2, t0, 1.0 * (C - TR), None, M.mult).then_inc(S["k1"], 1)
            V.tensor_scalar(t4, t1, TR - 1.0 * W, None, M.mult).then_inc(S["k1"], 1)
        elif k == 2:
            V.wait_ge(S["k1"], 2)
            V.tensor_tensor(t3, t4, t2, M.add).then_inc(S["k1"], 1)
        elif k == 3:
            V.wait_ge(S["k1"], 3)
            V.tensor_tensor(t0, pl, t3, M.add).then_inc(S["k2"], 1)
        else:
            V.wait_ge(S["k2"], 1)
            for u in range(4):
                V.tensor_copy(T.poff[32 * u:32 * u + 32, :], t0).then_inc(S["k3"], 1)

    for e, name in ((A, "A"), (V, "V")):
        for step in cfg[name].split():
            if step == "w":
                V.wait_ge(S["wl"], 16)
                V.quantize_mx(T.qw[:], T.sw[:], T.wb[:]).then_inc(S["pw"], 1)
            elif step == "v":
                V.wait_ge(S["vl"], 16)
                V.quantize_mx(T.qv[:], T.sv[:], T.vb[:]).then_inc(S["pv"], 1)
            elif step[0] == "p":
                pack(step[1])
            elif step[0] == "k":
                places(int(step[1]))
            elif step in message:
                repack(step)
            elif len(step) == 3:
                relu(e, step[0], step[1], int(step[2]))
            else:
                gather(e, step[0], int(step[1]))
    P.wait_ge(S["pw"], 1)
    for k in range(N + narrow):
        product(k)

    lands = {"X0": ("O", C), "X1": ("lF", C), "Y": ("lF", 0), "N": ("lN", 0), "O": ("O", 0)}
    sent = 0
    for step in cfg["G"].split():
        step, kinds = (step + ":qs").split(":")[:2]
        parts = []
        for name in ([step] if step in message else step):
            if name in "enl":
                a = role(r, name)
                g.wait_ge(S["px" + name], 1)
                parts.append((a, "ax%d" % r, "x", a * C, "lx", r * C, C))
            else:
                g.wait_ge(S["p" + name], 1)
                parts.append((message[name][0], "a" + name, name, message[name][4]) + lands[name] + (message[name][5],))
        for kind in kinds:
            trs = []
            for q, sem, src, c0, dst, at, n in parts:
                rid, pid = topo.addr(T.cores[q])[:2]
                u, v = T[kind + src][:, c0:c0 + n], T[kind + dst][:, at:at + n]
                if kind == "q":
                    u, v = u.bitcast(dt.uint8), v.bitcast(dt.uint8)
                trs.append(RemoteDMATransfer(dst_ids=[DstId(rid=rid, pnc=pid)], dma_engine_mask=sum(1 << e for e in eng[q]),
                                             remote_sem=S[sem], src=u, dst=v))
                sent += len(eng[q])
            g.remote_dma_fused(trs, local_sem=S["ls"])

    P.wait_ge(S["pv"], 1)
    for name in message:
        P.wait_ge(S["p" + name], 1)
    last = cfg["last"].split()
    goes = {"X0": fx * C + f0 * TR, "X1": fx * C + o0 * TR, "Y": fy * C, "N": near * C, "O": r * C}
    seen = {"O"}
    for k, step in enumerate(last):
        name, e = step[:-1], (V if step[-1] == "V" else A)
        (buf, c0), n = lands[name], message[name][5]
        lead = max(0, 128 - n)
        for u in ([name, "Y"] if name == "X1" else [name]):
            if u not in seen:
                P.wait_ge(S["a" + u], 2 * len(out))
                seen.add(u)
        P.matmul_mx(T.ps[:, 512 * k:512 * k + lead + n], T.qv[:], T.sv[:], T["q" + buf][:, c0 - lead:c0 + n],
                    T["s" + buf][:, c0 - lead:c0 + n], True, True).then_inc(S["y%d" % k], 1)
        e.wait_ge(S["y%d" % k], 1)
        src, dst = T.ps[:, 512 * k + lead:512 * k + lead + n], T.ysb[:, goes[name]:goes[name] + n]
        (V.tensor_copy(dst, src) if e is V else A.activation(dst, src, Copy)).then_inc(S["cp"], 1)
    for e in (V, A):
        e.wait_ge(S["k3"], 4)
        e.wait_ge(S["cp"], len(last))
    for j in range(2):
        a = 256 * j
        V.tensor_copy(T.yo[:, a:a + 128], T.ysb[:].indirect(T.poff[:, a // 16:a // 16 + 8])).then_inc(S["yd%d" % j], 1)
        A.activation(T.yo[:, a + 128:a + 256], T.ysb[:].indirect(T.poff[:, a // 16 + 8:a // 16 + 16]), Copy).then_inc(S["yd%d" % j], 1)
        g.sync.wait_ge(S["yd%d" % j], 2)
        g.sync.dma_start(T.y[:, a:a + 256], T.yo[:, a:a + 256]).then_inc(S["st"], 16)
    g.sync.wait_ge(S["st"], 32)
    g.wait_ge(S["ls"], sent)
